import numpy as np
import ml_dtypes


def mxq(x, axis, fmt="e4m3"):
    dtype, down = {"e4m3": (ml_dtypes.float8_e4m3fn, 7), "e5m2": (ml_dtypes.float8_e5m2, 14)}[fmt]
    v = np.moveaxis(np.asarray(x, np.float32).astype(ml_dtypes.bfloat16).astype(np.float64), axis, -1)
    blocks = v.reshape(v.shape[:-1] + (-1, 32))
    amax = np.abs(blocks).max(-1, keepdims=True)
    byte = np.maximum(np.where(amax > 0, np.frexp(amax)[1] - 1 + 127, 0) - down, 1)
    scale = np.exp2(byte - 127.0)
    codes = (blocks / scale).astype(np.float32).astype(dtype).astype(np.float64)
    return np.moveaxis((codes * scale).reshape(v.shape), -1, axis)


WIDE = False


def mx_kscale(k):
    if not WIDE:
        return np.ones(k)
    levels = np.array([30, -30])
    if k % 512:
        return np.exp2(np.random.permutation(np.resize(levels, k // 32))).repeat(32)
    a = np.empty((k // 512, 16))
    for p in range(k // 512):
        a[p, :8] = np.random.permutation(np.resize(levels, 8))
        for g in range(8):
            far = levels[np.abs(levels - a[p, g]) >= 10]
            a[p, g + 8] = far[np.random.randint(len(far))]
    return np.exp2(a.ravel()).repeat(32)


def f64(x):
    return np.asarray(x).astype(np.float64)


def striped(idx):
    return np.tile(np.asarray(idx).reshape(-1, 16).T, (8, 1)).astype(np.uint16)


def unstriped(offs):
    return offs[:16].T.reshape(-1).astype(np.int64)


E2M1 = np.array([0.0, 0.5, 1.0, 1.5, 2.0, 3.0, 4.0, 6.0, -0.0, -0.5, -1.0, -1.5, -2.0, -3.0, -4.0, -6.0])


def pack_weight(w, fmt):
    k, n = w.shape
    w = f64(np.asarray(w, np.float32).astype(ml_dtypes.bfloat16)).reshape(k // 32, 32, n)
    amax = np.abs(w).max(1)
    if fmt in ("e4m3", "e5m2"):
        byte = np.frexp(amax)[1] - 1 + 127 - (7 if fmt == "e4m3" else 14)
    else:
        mant, ex = np.frexp(amax / 6.0)
        byte = np.where(mant > 0.5, ex, ex - 1) + 127
    byte = np.clip(np.where(amax > 0, byte, 1), 1, 254)
    scaled = (w * np.exp2(127.0 - byte)[:, None, :]).reshape(k, n).astype(np.float32)
    by_word = np.ascontiguousarray(scaled.reshape(k // 512, 128, 4, n).transpose(0, 1, 3, 2))
    if fmt in ("e4m3", "e5m2"):
        words = by_word.astype(ml_dtypes.float8_e4m3fn if fmt == "e4m3" else ml_dtypes.float8_e5m2).view(np.uint8)
    else:
        c = by_word.astype(ml_dtypes.float4_e2m1fn).view(np.uint8) & 0xF
        words = (c[..., 0::2] | (c[..., 1::2] << 4)).reshape(k // 512, 128, 2 * n)
    return np.ascontiguousarray(words), np.ascontiguousarray(byte.astype(np.uint8).reshape(k // 512, 16, n))


def unpack_weight(words, scales, fmt):
    g, _, n = scales.shape
    words = np.ascontiguousarray(words).reshape(g, 128, n, -1)
    if fmt in ("e4m3", "e5m2"):
        vals = words.view(ml_dtypes.float8_e4m3fn if fmt == "e4m3" else ml_dtypes.float8_e5m2).astype(np.float64)
    else:
        nib = np.empty((g, 128, n, 4), np.uint8)
        nib[..., 0::2] = words & 0xF
        nib[..., 1::2] = words >> 4
        vals = E2M1[nib]
    vals = vals * np.repeat(np.exp2(scales.astype(np.float64) - 127.0), 8, axis=1)[..., None]
    return vals.transpose(0, 1, 3, 2).reshape(g * 512, n)


K, T, J, R, V, M, Q, O, U, X, D, N, E = 512, 1024, 256, 512, 1024, 512, 128, 64, 64, 128, 256, 256, 512


def setup_inputs():
    n = np.random.standard_normal
    idx = np.random.permutation(V)[:R]
    idx2 = np.random.permutation(T)[:J]
    idx3 = np.random.permutation(J)[:O]
    idx4 = np.random.permutation(J)[:U]
    idx5 = np.random.permutation(T)[:D]
    idx6 = np.random.permutation(E)[:D]
    idx7 = np.random.permutation(E)[:D]
    fk = mx_kscale(K)
    fm = mx_kscale(M)
    fr = mx_kscale(R)
    xtp = pack_weight(n((K, T)) / fk[:, None], "e5m2")
    wtp = pack_weight(n((K, V)) * 1 / np.sqrt(K) * fk[:, None], "e2m1")
    xcp = pack_weight(n((M, Q)) / fm[:, None], "e5m2")
    wgp = pack_weight(n((M, R)) * 1 / np.sqrt(M) * fm[:, None] * fr, "e4m3")
    wbp = pack_weight(n((R, N)) * 1 / np.sqrt(R) / fr[:, None], "e2m1")
    wsp = pack_weight(n((K, N)) * 1 / np.sqrt(K) * fk[:, None], "e2m1")
    return {
        "xt_words": xtp[0],
        "xt_scales": xtp[1],
        "wt_words": wtp[0],
        "wt_scales": wtp[1],
        "xc_words": xcp[0],
        "xc_scales": xcp[1],
        "wg_words": wgp[0],
        "wg_scales": wgp[1],
        "wb_words": wbp[0],
        "wb_scales": wbp[1],
        "ws_words": wsp[0],
        "ws_scales": wsp[1],
        "offs": striped(idx),
        "offs2": striped(idx2),
        "offs3": striped(idx3),
        "offs4": striped(idx4),
        "offs5": striped(idx5),
        "offs6": striped(idx6),
        "offs7": striped(idx7),
    }


def reference(xt_words, xt_scales, wt_words, wt_scales, xc_words, xc_scales, wg_words, wg_scales, wb_words, wb_scales, ws_words, ws_scales, offs, offs2, offs3, offs4, offs5, offs6, offs7):
    idx = unstriped(offs)
    idx2 = unstriped(offs2)
    idx3 = unstriped(offs3)
    idx4 = unstriped(offs4)
    idx5 = unstriped(offs5)
    idx6 = unstriped(offs6)
    idx7 = unstriped(offs7)
    xtu = unpack_weight(xt_words, xt_scales, "e5m2")
    wtu = unpack_weight(wt_words, wt_scales, "e2m1")
    xcu = unpack_weight(xc_words, xc_scales, "e5m2")
    wgu = unpack_weight(wg_words, wg_scales, "e4m3")
    wbu = unpack_weight(wb_words, wb_scales, "e2m1")
    wsu = unpack_weight(ws_words, ws_scales, "e2m1")
    wtidxg = wtu[:, idx]
    xtidx2g = xtu[:, idx2]
    a = wtidxg.T @ xtidx2g
    g0 = wgu.T @ xcu
    ga = g0[:, 0:1]
    gb = g0[:, 64:65]
    h1 = a[:, idx3] * ga
    h2 = a[:, idx4] * gb
    h3 = np.concatenate([h1, h2], axis=1)
    hid = np.concatenate([h3, g0], axis=1)
    hidq = mxq(hid, 0, "e4m3")
    xtidx5g = xtu[:, idx5]
    p = wbu.T @ hidq + wsu.T @ xtidx5g
    pa = np.zeros((N, E))
    pa[:, idx6] = p
    pb = np.zeros((N, E))
    pb[:, idx7] = p
    y = pa + pb
    return y

@@ -1,0 +1,234 @@
+from contextlib import ExitStack
+
+import concourse.mybir as mybir
+from concourse.masks import make_identity
+
+K, T, J, R, V, M, Q, O, U, X, D, N, E = 512, 1024, 256, 512, 1024, 512, 128, 64, 64, 128, 256, 256, 512
+FLOPS = 2 * (K * R * J + M * R * Q + R * N * D + K * N * D)
+
+F32 = mybir.dt.float32
+BF16 = mybir.dt.bfloat16
+I32 = mybir.dt.int32
+U32 = mybir.dt.uint32
+U16 = mybir.dt.uint16
+U8 = mybir.dt.uint8
+E4M3 = mybir.dt.float8_e4m3fn_x4
+E5M2 = mybir.dt.float8_e5m2_x4
+E2M1 = mybir.dt.float4_e2m1fn_x4
+COPY = mybir.ActivationFunctionType.Copy
+ADD = mybir.AluOpType.add
+
+P = 128
+PACK = 4
+QUADS = 4
+ALIGN = 64
+CTX = Q
+
+
+def tile_list_ctxthirds_chosen_further_pagetwice_kernel(
+    tc, xt_words, xt_scales, wt_words, wt_scales, xc_words, xc_scales, wg_words, wg_scales,
+    wb_words, wb_scales, ws_words, ws_scales, offs, offs2, offs3, offs4, offs5, offs6, offs7, out,
+):
+    nc = tc.nc
+    with ExitStack() as ctx:
+        sb = ctx.enter_context(tc.tile_pool(name="sb", bufs=1))
+        ps = ctx.enter_context(tc.psum_pool(name="ps", bufs=1))
+
+        def tile(name, shape, dtype):
+            return sb.tile(shape, dtype, name=name, align_bytes=ALIGN)
+
+        def load_list(name, src):
+            lst = tile(name, list(src.shape), U16)
+            nc.sync.dma_start(lst[:], src)
+            return lst
+
+        def words8(src):
+            return src[0].rearrange("p c b -> p (c b)").bitcast(I32)
+
+        def words4(src):
+            return src[0].bitcast(I32)
+
+        def load_rows(queue, plane, src, g):
+            queue.dma_start(plane[32 * g : 32 * g + 4, :].bitcast(I32), src[0, 4 * g : 4 * g + 4, :].bitcast(I32))
+
+        def load_halved(queue, plane, first, src, g):
+            rows = src[0].rearrange("(u g r) c -> g r u c", u=2, g=2).bitcast(I32)
+            queue.dma_start(plane[32 * g : 32 * g + 4, :, first : first + src.shape[2]].bitcast(I32), rows[g])
+
+        def lift(plane):
+            nc.vector.tensor_copy(plane[64:128, 0, :].bitcast(I32), plane[0:64, 1, :].bitcast(I32))
+
+        def stage_rows(queue, stage, first, src):
+            words = src.shape[2] // 4
+            queue.dma_start(stage[:, :, first : first + words], src[0].rearrange("(g r) c -> r g c", r=4).bitcast(I32))
+
+        def spread(plane, stage):
+            for g in range(QUADS):
+                nc.vector.tensor_copy(plane[32 * g : 32 * g + 4, 0, :].bitcast(I32), stage[:, g, :])
+
+        def pick_words(picked, entries):
+            nc.vector.tensor_copy(picked[0][:], xt_w[:].indirect(entries))
+
+        def pick_scales(picked, entries):
+            nc.vector.tensor_copy(picked[1][:], xt_plane[:].indirect(entries))
+
+        def quantise(name, hid, tag):
+            codes = sb.tile([P, P], U32, name=f"{name}_codes", tag=tag, align_bytes=ALIGN)
+            plane = tile(f"{name}_scales", [P, P], U8)
+            nc.vector.quantize_mx(codes[:].bitcast(E4M3), plane[:], hid[:].rearrange("p c t -> p (c t)"))
+            return codes, plane
+
+        def short_way(dst, h, picked):
+            nc.tensor.matmul_mx(dst, lhsT=ws_w[:, P * h : P * (h + 1)].bitcast(E2M1),
+                                lhsT_scale=out_plane[:, 0, N + P * h : N + P * (h + 1)],
+                                rhs=picked[0][:].bitcast(E5M2), rhs_scale=picked[1][:], start=True, stop=False)
+
+        def output_matrix(dst, h, quantised):
+            codes, plane = quantised
+            nc.tensor.matmul_mx(dst, lhsT=wb_w[:, P * h : P * (h + 1)].bitcast(E2M1),
+                                lhsT_scale=out_plane[:, 0, P * h : P * (h + 1)],
+                                rhs=codes[:].bitcast(E4M3), rhs_scale=plane[:], start=False, stop=True)
+
+        def fetch(a_t, t):
+            nc.scalar.activation(h3[:, t, 0:O], a_t[:].indirect(lst3[:]), COPY, scale=gains[:, 2 * t : 2 * t + 1])
+            nc.scalar.activation(h3[:, t, O:X], a_t[:].indirect(lst4[:]), COPY, scale=gains[:, 2 * t + 1 : 2 * t + 2])
+
+        def put_v(page, entries, values):
+            nc.vector.tensor_copy(page[:].indirect(entries), values)
+
+        def put_s(page, entries, values):
+            nc.scalar.activation(page[:].indirect(entries), values, COPY)
+
+        wt_plane = tile("wt_plane", [P, V], U8)
+        xt_plane = tile("xt_plane", [P, T], U8)
+        ctx_plane = tile("ctx_plane", [P, 1, Q + R], U8)
+        out_plane = tile("out_plane", [P, 2, 2 * N], U8)
+        ctx_stage = tile("ctx_stage", [4, QUADS, (Q + R) // 4], I32)
+        ident = tile("ident", [P, P], F32)
+        wt_w = tile("wt_w", [P, V], U16)
+        xt_w = tile("xt_w", [P, T], U32)
+        xc_w = tile("xc_w", [P, Q], U32)
+        wg_w = tile("wg_w", [P, R], U32)
+        wb_w = tile("wb_w", [P, N], U16)
+        ws_w = tile("ws_w", [P, N], U16)
+        pages = {(name, h): tile(f"page_{name}{h}", [P, E], F32) for name in ("a", "b") for h in range(2)}
+        late, early = slice(0, X // 16), slice(X // 16, D // 16)
+        wt_g = tile("wt_g", [P, R], U16)
+        wt_d = [tile(f"wt_d{u}", [P, 2, P], U16) for u in range(2)]
+        wt_gs = tile("wt_gs", [P, PACK, P], U8)
+        g0t = tile("g0t", [P, PACK, P], F32)
+        hid_ctx = tile("hid_ctx", [P, Q, PACK], BF16)
+        gains = tile("gains", [P, PACK * 2], F32)
+        x2 = (tile("x2_w", [P, J], U32), tile("x2_s", [P, J], U8))
+        x5 = (tile("x5_w", [P, D], U32), tile("x5_s", [P, D], U8))
+        h3 = tile("h3", [P, PACK, X], F32)
+        hid_pl = tile("hid_pl", [P, X, PACK], BF16)
+        total = [tile(f"total{h}", [P, E], F32) for h in range(2)]
+
+        nc.vector.memset(wt_plane[:].bitcast(I32), 0)
+        nc.vector.memset(xt_plane[:].bitcast(I32), 0)
+        nc.vector.memset(ctx_plane[:].rearrange("p u c -> p (u c)").bitcast(I32), 0)
+        nc.vector.memset(out_plane[:].rearrange("p u c -> p (u c)").bitcast(I32), 0)
+        lst1 = load_list("lst1", offs)
+        stage_rows(nc.scalar, ctx_stage, 0 // 4, xc_scales)
+        nc.sync.dma_start(wt_w[:].bitcast(I32), words4(wt_words))
+        stage_rows(nc.scalar, ctx_stage, CTX // 4, wg_scales)
+        nc.sync.dma_start(xc_w[:].bitcast(I32), words8(xc_words))
+        load_rows(nc.scalar, wt_plane, wt_scales, 0)
+        nc.sync.dma_start(wg_w[:].bitcast(I32), words8(wg_words))
+        load_rows(nc.scalar, wt_plane, wt_scales, 1)
+        make_identity(nc, ident[:])
+        lst2 = load_list("lst2", offs2)
+        load_rows(nc.scalar, wt_plane, wt_scales, 2)
+        load_rows(nc.sync, xt_plane, xt_scales, 0)
+        load_rows(nc.scalar, wt_plane, wt_scales, 3)
+        load_rows(nc.sync, xt_plane, xt_scales, 1)
+        load_rows(nc.sync, xt_plane, xt_scales, 2)
+        nc.sync.dma_start(xt_w[:].bitcast(I32), words8(xt_words))
+        load_halved(nc.sync, out_plane, 0, wb_scales, 0)
+        load_halved(nc.sync, out_plane, 0, wb_scales, 1)
+        load_halved(nc.sync, out_plane, N, ws_scales, 0)
+        load_halved(nc.sync, out_plane, N, ws_scales, 1)
+        load_rows(nc.sync, xt_plane, xt_scales, 3)
+        lst5 = load_list("lst5", offs5)
+        nc.sync.dma_start(wb_w[:].bitcast(I32), words4(wb_words))
+        nc.sync.dma_start(ws_w[:].bitcast(I32), words4(ws_words))
+        lst3 = load_list("lst3", offs3)
+        lst4 = load_list("lst4", offs4)
+        lst7 = load_list("lst7", offs7)
+        lst6 = load_list("lst6", offs6)
+        nc.vector.memset(pages["a", 0][:], 0.0)
+        nc.vector.memset(pages["a", 1][:], 0.0)
+        nc.vector.memset(pages["b", 0][:], 0.0)
+        nc.vector.memset(pages["b", 1][:], 0.0)
+        spread(ctx_plane, ctx_stage)
+        nc.vector.tensor_copy(wt_g[:], wt_w[:].indirect(lst1[:]))
+        for u in range(2):
+            nc.vector.tensor_copy(wt_d[u][:], wt_g[:].rearrange("p (c u t) -> p u t c", u=2, t=2)[:, u])
+        nc.vector.tensor_copy(wt_gs[:].rearrange("p t c -> p c t"), wt_plane[:].indirect(lst1[:]))
+        g0t_ps = ps.tile([P, R], F32, name="g0t_ps", tag="bank_early")
+        nc.tensor.matmul_mx(g0t_ps[:], lhsT=xc_w[:].bitcast(E5M2), lhsT_scale=ctx_plane[:, 0, 0:Q],
+                            rhs=wg_w[:].bitcast(E4M3), rhs_scale=ctx_plane[:, 0, Q : Q + R], start=True, stop=True)
+        nc.scalar.activation(g0t[:], g0t_ps[:].rearrange("q (c t) -> q t c", t=PACK), COPY)
+        g0_ps = ps.tile([P, PACK, Q], F32, name="g0_ps")
+        for t in range(PACK):
+            nc.tensor.transpose(g0_ps[:, t, :], g0t[:, t, :], ident[:])
+        nc.scalar.copy(gains[:].rearrange("p (t s) -> p t s", s=2), g0_ps[:, :, 0:Q:64])
+        nc.scalar.copy(hid_ctx[:], g0_ps[:].rearrange("p t q -> p q t"))
+        lift(out_plane)
+        pick_words(x2, lst2[:])
+        pick_scales(x2, lst2[:])
+        a_ps = []
+        for t in range(PACK):
+            bank = ps.tile([P, J], F32, name=f"a_ps{t}", tag=f"bank_a{t}")
+            nc.tensor.matmul_mx(bank[:], lhsT=wt_d[t // 2][:, t % 2, :].bitcast(E2M1), lhsT_scale=wt_gs[:, t, :],
+                                rhs=x2[0][:].bitcast(E5M2), rhs_scale=x2[1][:], start=True, stop=True)
+            a_ps.append(bank)
+        pick_words(x5, lst5[:])
+        pick_scales(x5, lst5[:])
+        x5l = (x5[0][:, 0:X], x5[1][:, 0:X])
+        x5e = (x5[0][:, X:D], x5[1][:, X:D])
+        ctx_q = quantise("ctx", hid_ctx, "wt_d0")
+        pe_ps = ps.tile([P, 2, P], F32, name="pe_ps", tag="bank_early")
+        for h in range(2):
+            short_way(pe_ps[:, h, :], h, x5e)
+            output_matrix(pe_ps[:, h, :], h, ctx_q)
+        pl_ps = [ps.tile([P, X], F32, name=f"pl_ps{h}") for h in range(2)]
+        for h in range(2):
+            short_way(pl_ps[h][:], h, x5l)
+        a0 = sb.tile([P, J], F32, name="a0", tag="rows0", align_bytes=ALIGN)
+        nc.scalar.copy(a0[:], a_ps[0][:])
+        fetch(a0, 0)
+        a1 = sb.tile([P, J], F32, name="a1", tag="rows1", align_bytes=ALIGN)
+        nc.scalar.copy(a1[:], a_ps[1][:])
+        fetch(a1, 1)
+        a2 = sb.tile([P, J], F32, name="a2", tag="rows2", align_bytes=ALIGN)
+        nc.vector.tensor_copy(a2[:], a_ps[2][:])
+        fetch(a2, 2)
+        a3 = sb.tile([P, J], F32, name="a3", tag="rows3", align_bytes=ALIGN)
+        nc.vector.tensor_copy(a3[:], a_ps[3][:])
+        fetch(a3, 3)
+        p_e = tile("p_e", [P, 2, P], F32)
+        nc.vector.tensor_copy(p_e[:], pe_ps[:])
+        p_e0 = p_e[:, 0, :]
+        p_e1 = p_e[:, 1, :]
+        nc.vector.tensor_copy(hid_pl[:], h3[:].rearrange("p t x -> p x t"))
+        pl_q = quantise("pl", hid_pl, "pl_codes")
+        put_v(pages["a", 0], lst6[:, early], p_e0[:])
+        put_s(pages["b", 0], lst7[:, early], p_e0[:])
+        put_s(pages["b", 1], lst7[:, early], p_e1[:])
+        put_s(pages["a", 1], lst6[:, early], p_e1[:])
+        for h in range(2):
+            output_matrix(pl_ps[h][:], h, pl_q)
+        p_l0 = sb.tile([P, P], F32, name="p_l0", tag="p_l0", align_bytes=ALIGN)
+        nc.vector.tensor_copy(p_l0[:], pl_ps[0][:])
+        p_l1 = sb.tile([P, P], F32, name="p_l1", tag="p_l1", align_bytes=ALIGN)
+        nc.vector.tensor_copy(p_l1[:], pl_ps[1][:])
+        put_v(pages["a", 0], lst6[:, late], p_l0[:])
+        put_s(pages["b", 0], lst7[:, late], p_l0[:])
+        put_v(pages["a", 1], lst6[:, late], p_l1[:])
+        put_s(pages["b", 1], lst7[:, late], p_l1[:])
+        nc.vector.tensor_tensor(total[0][:], pages["a", 0][:], pages["b", 0][:], ADD)
+        nc.sync.dma_start(out[P * 0 : P * 1, :], total[0][:])
+        nc.vector.tensor_tensor(total[1][:], pages["a", 1][:], pages["b", 1][:], ADD)
+        nc.sync.dma_start(out[P * 1 : P * 2, :], total[1][:])

@@ -121,7 +121,7 @@ def tile_list_ctxthirds_chosen_further_pagetwice_kernel(
         gains = tile("gains", [P, PACK * 2], F32)
         x2 = (tile("x2_w", [P, J], U32), tile("x2_s", [P, J], U8))
         x5 = (tile("x5_w", [P, D], U32), tile("x5_s", [P, D], U8))
-        h3 = tile("h3", [P, PACK, X], F32)
+        h3 = [tile(f"h3{u}", [P, PACK, O], F32) for u in range(2)]
         hid_pl = tile("hid_pl", [P, X, PACK], BF16)
         total = [tile(f"total{h}", [P, E], F32) for h in range(2)]
 
@@ -130,9 +130,9 @@ def tile_list_ctxthirds_chosen_further_pagetwice_kernel(
         nc.vector.memset(ctx_plane[:].rearrange("p u c -> p (u c)").bitcast(I32), 0)
         nc.vector.memset(out_plane[:].rearrange("p u c -> p (u c)").bitcast(I32), 0)
         lst1 = load_list("lst1", offs)
-        stage_rows(nc.scalar, ctx_stage, 0 // 4, xc_scales)
-        nc.sync.dma_start(wt_w[:].bitcast(I32), words4(wt_words))
         stage_rows(nc.scalar, ctx_stage, CTX // 4, wg_scales)
+        nc.sync.dma_start(wt_w[:].bitcast(I32), words4(wt_words))
+        stage_rows(nc.scalar, ctx_stage, 0 // 4, xc_scales)
         nc.sync.dma_start(xc_w[:].bitcast(I32), words8(xc_words))
         load_rows(nc.scalar, wt_plane, wt_scales, 0)
         nc.sync.dma_start(wg_w[:].bitcast(I32), words8(wg_words))
@@ -198,22 +198,25 @@ def tile_list_ctxthirds_chosen_further_pagetwice_kernel(
             short_way(pl_ps[h][:], h, x5l)
         a0 = sb.tile([P, J], F32, name="a0", tag="rows0", align_bytes=ALIGN)
         nc.scalar.copy(a0[:], a_ps[0][:])
-        fetch(a0, 0)
         a1 = sb.tile([P, J], F32, name="a1", tag="rows1", align_bytes=ALIGN)
         nc.scalar.copy(a1[:], a_ps[1][:])
-        fetch(a1, 1)
         a2 = sb.tile([P, J], F32, name="a2", tag="rows2", align_bytes=ALIGN)
         nc.vector.tensor_copy(a2[:], a_ps[2][:])
-        fetch(a2, 2)
         a3 = sb.tile([P, J], F32, name="a3", tag="rows3", align_bytes=ALIGN)
         nc.vector.tensor_copy(a3[:], a_ps[3][:])
-        fetch(a3, 3)
+        for t, a_t in enumerate((a0, a1, a2, a3)):
+            nc.scalar.activation(h3[0][:, t, :], a_t[:].indirect(lst3[:]), COPY, scale=gains[:, 2 * t : 2 * t + 1])
+        for t, a_t in enumerate((a0, a1, a2, a3)):
+            nc.scalar.activation(h3[1][:, t, :], a_t[:].indirect(lst4[:]), COPY, scale=gains[:, 2 * t + 1 : 2 * t + 2])
         p_e = tile("p_e", [P, 2, P], F32)
         nc.vector.tensor_copy(p_e[:], pe_ps[:])
         p_e0 = p_e[:, 0, :]
         p_e1 = p_e[:, 1, :]
-        nc.vector.tensor_copy(hid_pl[:], h3[:].rearrange("p t x -> p x t"))
-        pl_q = quantise("pl", hid_pl, "pl_codes")
+        nc.vector.tensor_copy(hid_pl[:, 0:O, :], h3[0][:].rearrange("p t x -> p x t"))
+        pl_q = (tile("pl_codes", [P, P], U32), tile("pl_scales", [P, P], U8))
+        nc.vector.quantize_mx(pl_q[0][:, 0:O].bitcast(E4M3), pl_q[1][:, 0:O], hid_pl[:, 0:O, :].rearrange("p c t -> p (c t)"))
+        nc.vector.tensor_copy(hid_pl[:, O:X, :], h3[1][:].rearrange("p t x -> p x t"))
+        nc.vector.quantize_mx(pl_q[0][:, O:X].bitcast(E4M3), pl_q[1][:, O:X], hid_pl[:, O:X, :].rearrange("p c t -> p (c t)"))
         put_v(pages["a", 0], lst6[:, early], p_e0[:])
         put_s(pages["b", 0], lst7[:, early], p_e0[:])
         put_s(pages["b", 1], lst7[:, early], p_e1[:])
@@ -230,5 +233,6 @@ def tile_list_ctxthirds_chosen_further_pagetwice_kernel(
         put_s(pages["b", 1], lst7[:, late], p_l1[:])
         nc.vector.tensor_tensor(total[0][:], pages["a", 0][:], pages["b", 0][:], ADD)
         nc.sync.dma_start(out[P * 0 : P * 1, :], total[0][:])
-        nc.vector.tensor_tensor(total[1][:], pages["a", 1][:], pages["b", 1][:], ADD)
-        nc.sync.dma_start(out[P * 1 : P * 2, :], total[1][:])
+        for cols in (slice(0, E // 2), slice(E // 2, E)):
+            nc.vector.tensor_tensor(total[1][:, cols], pages["a", 1][:, cols], pages["b", 1][:, cols], ADD)
+            nc.sync.dma_start(out[P : 2 * P, cols], total[1][:, cols])

@@ -142,9 +142,9 @@ def tile_list_ctxthirds_chosen_further_pagetwice_kernel(
         load_rows(nc.scalar, wt_plane, wt_scales, 2)
         load_rows(nc.sync, xt_plane, xt_scales, 0)
         load_rows(nc.scalar, wt_plane, wt_scales, 3)
+        nc.sync.dma_start(xt_w[:].bitcast(I32), words8(xt_words))
         load_rows(nc.sync, xt_plane, xt_scales, 1)
         load_rows(nc.sync, xt_plane, xt_scales, 2)
-        nc.sync.dma_start(xt_w[:].bitcast(I32), words8(xt_words))
         load_halved(nc.sync, out_plane, 0, wb_scales, 0)
         load_halved(nc.sync, out_plane, 0, wb_scales, 1)
         load_halved(nc.sync, out_plane, N, ws_scales, 0)
@@ -231,8 +231,7 @@ def tile_list_ctxthirds_chosen_further_pagetwice_kernel(
         put_s(pages["b", 0], lst7[:, late], p_l0[:])
         put_v(pages["a", 1], lst6[:, late], p_l1[:])
         put_s(pages["b", 1], lst7[:, late], p_l1[:])
-        nc.vector.tensor_tensor(total[0][:], pages["a", 0][:], pages["b", 0][:], ADD)
-        nc.sync.dma_start(out[P * 0 : P * 1, :], total[0][:])
-        for cols in (slice(0, E // 2), slice(E // 2, E)):
-            nc.vector.tensor_tensor(total[1][:, cols], pages["a", 1][:, cols], pages["b", 1][:, cols], ADD)
-            nc.sync.dma_start(out[P : 2 * P, cols], total[1][:, cols])
+        for h in range(2):
+            for cols in (slice(0, E // 2), slice(E // 2, E)):
+                nc.vector.tensor_tensor(total[h][:, cols], pages["a", h][:, cols], pages["b", h][:, cols], ADD)
+                nc.sync.dma_start(out[P * h : P * (h + 1), cols], total[h][:, cols])

from contextlib import ExitStack

import concourse.mybir as mybir
from concourse.masks import make_identity

K, T, J, R, V, M, Q, O, U, X, D, N, E = 512, 1024, 256, 512, 1024, 512, 128, 64, 64, 128, 256, 256, 512
FLOPS = 2 * (K * R * J + M * R * Q + R * N * D + K * N * D)

F32 = mybir.dt.float32
BF16 = mybir.dt.bfloat16
I32 = mybir.dt.int32
U32 = mybir.dt.uint32
U16 = mybir.dt.uint16
U8 = mybir.dt.uint8
E4M3 = mybir.dt.float8_e4m3fn_x4
E5M2 = mybir.dt.float8_e5m2_x4
E2M1 = mybir.dt.float4_e2m1fn_x4
COPY = mybir.ActivationFunctionType.Copy
ADD = mybir.AluOpType.add

P = 128
PACK = 4
QUADS = 4
ALIGN = 64
CTX = Q


def tile_list_ctxthirds_chosen_further_pagetwice_kernel(
    tc, xt_words, xt_scales, wt_words, wt_scales, xc_words, xc_scales, wg_words, wg_scales,
    wb_words, wb_scales, ws_words, ws_scales, offs, offs2, offs3, offs4, offs5, offs6, offs7, out,
):
    nc = tc.nc
    with ExitStack() as ctx:
        sb = ctx.enter_context(tc.tile_pool(name="sb", bufs=1))
        ps = ctx.enter_context(tc.psum_pool(name="ps", bufs=1))

        def tile(name, shape, dtype):
            return sb.tile(shape, dtype, name=name, align_bytes=ALIGN)

        def load_list(name, src):
            lst = tile(name, list(src.shape), U16)
            nc.sync.dma_start(lst[:], src)
            return lst

        def words8(src):
            return src[0].rearrange("p c b -> p (c b)").bitcast(I32)

        def words4(src):
            return src[0].bitcast(I32)

        def load_rows(queue, plane, src, g):
            queue.dma_start(plane[32 * g : 32 * g + 4, :].bitcast(I32), src[0, 4 * g : 4 * g + 4, :].bitcast(I32))

        def load_halved(queue, plane, first, src, g):
            rows = src[0].rearrange("(u g r) c -> g r u c", u=2, g=2).bitcast(I32)
            queue.dma_start(plane[32 * g : 32 * g + 4, :, first : first + src.shape[2]].bitcast(I32), rows[g])

        def lift(plane):
            nc.vector.tensor_copy(plane[64:128, 0, :].bitcast(I32), plane[0:64, 1, :].bitcast(I32))

        def stage_rows(queue, stage, first, src):
            words = src.shape[2] // 4
            queue.dma_start(stage[:, :, first : first + words], src[0].rearrange("(g r) c -> r g c", r=4).bitcast(I32))

        def spread(plane, stage):
            for g in range(QUADS):
                nc.vector.tensor_copy(plane[32 * g : 32 * g + 4, 0, :].bitcast(I32), stage[:, g, :])

        def pick_words(picked, entries):
            nc.vector.tensor_copy(picked[0][:], xt_w[:].indirect(entries))

        def pick_scales(picked, entries):
            nc.vector.tensor_copy(picked[1][:], xt_plane[:].indirect(entries))

        def quantise(name, hid, tag):
            codes = sb.tile([P, P], U32, name=f"{name}_codes", tag=tag, align_bytes=ALIGN)
            plane = tile(f"{name}_scales", [P, P], U8)
            nc.vector.quantize_mx(codes[:].bitcast(E4M3), plane[:], hid[:].rearrange("p c t -> p (c t)"))
            return codes, plane

        def short_way(dst, h, picked):
            nc.tensor.matmul_mx(dst, lhsT=ws_w[:, P * h : P * (h + 1)].bitcast(E2M1),
                                lhsT_scale=out_plane[:, 0, N + P * h : N + P * (h + 1)],
                                rhs=picked[0][:].bitcast(E5M2), rhs_scale=picked[1][:], start=True, stop=False)

        def output_matrix(dst, h, quantised):
            codes, plane = quantised
            nc.tensor.matmul_mx(dst, lhsT=wb_w[:, P * h : P * (h + 1)].bitcast(E2M1),
                                lhsT_scale=out_plane[:, 0, P * h : P * (h + 1)],
                                rhs=codes[:].bitcast(E4M3), rhs_scale=plane[:], start=False, stop=True)

        def fetch(a_t, t):
            nc.scalar.activation(h3[:, t, 0:O], a_t[:].indirect(lst3[:]), COPY, scale=gains[:, 2 * t : 2 * t + 1])
            nc.scalar.activation(h3[:, t, O:X], a_t[:].indirect(lst4[:]), COPY, scale=gains[:, 2 * t + 1 : 2 * t + 2])

        def put_v(page, entries, values):
            nc.vector.tensor_copy(page[:].indirect(entries), values)

        def put_s(page, entries, values):
            nc.scalar.activation(page[:].indirect(entries), values, COPY)

        wt_plane = tile("wt_plane", [P, V], U8)
        xt_plane = tile("xt_plane", [P, T], U8)
        ctx_plane = tile("ctx_plane", [P, 1, Q + R], U8)
        out_plane = tile("out_plane", [P, 2, 2 * N], U8)
        ctx_stage = tile("ctx_stage", [4, QUADS, (Q + R) // 4], I32)
        ident = tile("ident", [P, P], F32)
        wt_w = tile("wt_w", [P, V], U16)
        xt_w = tile("xt_w", [P, T], U32)
        xc_w = tile("xc_w", [P, Q], U32)
        wg_w = tile("wg_w", [P, R], U32)
        wb_w = tile("wb_w", [P, N], U16)
        ws_w = tile("ws_w", [P, N], U16)
        pages = {(name, h): tile(f"page_{name}{h}", [P, E], F32) for name in ("a", "b") for h in range(2)}
        late, early = slice(0, X // 16), slice(X // 16, D // 16)
        wt_g = tile("wt_g", [P, R], U16)
        wt_d = [tile(f"wt_d{u}", [P, 2, P], U16) for u in range(2)]
        wt_gs = tile("wt_gs", [P, PACK, P], U8)
        g0t = tile("g0t", [P, PACK, P], F32)
        hid_ctx = tile("hid_ctx", [P, Q, PACK], BF16)
        gains = tile("gains", [P, PACK * 2], F32)
        x2 = (tile("x2_w", [P, J], U32), tile("x2_s", [P, J], U8))
        x5 = (tile("x5_w", [P, D], U32), tile("x5_s", [P, D], U8))
        h3 = [tile(f"h3{u}", [P, PACK, O], F32) for u in range(2)]
        hid_pl = tile("hid_pl", [P, X, PACK], BF16)
        total = [tile(f"total{h}", [P, E], F32) for h in range(2)]

        nc.vector.memset(wt_plane[:].bitcast(I32), 0)
        nc.vector.memset(xt_plane[:].bitcast(I32), 0)
        nc.vector.memset(ctx_plane[:].rearrange("p u c -> p (u c)").bitcast(I32), 0)
        nc.vector.memset(out_plane[:].rearrange("p u c -> p (u c)").bitcast(I32), 0)
        lst1 = load_list("lst1", offs)
        stage_rows(nc.scalar, ctx_stage, CTX // 4, wg_scales)
        nc.sync.dma_start(wt_w[:].bitcast(I32), words4(wt_words))
        stage_rows(nc.scalar, ctx_stage, 0 // 4, xc_scales)
        nc.sync.dma_start(xc_w[:].bitcast(I32), words8(xc_words))
        load_rows(nc.scalar, wt_plane, wt_scales, 0)
        nc.sync.dma_start(wg_w[:].bitcast(I32), words8(wg_words))
        load_rows(nc.scalar, wt_plane, wt_scales, 1)
        make_identity(nc, ident[:])
        lst2 = load_list("lst2", offs2)
        load_rows(nc.scalar, wt_plane, wt_scales, 2)
        load_rows(nc.sync, xt_plane, xt_scales, 0)
        load_rows(nc.scalar, wt_plane, wt_scales, 3)
        nc.sync.dma_start(xt_w[:].bitcast(I32), words8(xt_words))
        load_rows(nc.sync, xt_plane, xt_scales, 1)
        load_rows(nc.sync, xt_plane, xt_scales, 2)
        load_halved(nc.sync, out_plane, 0, wb_scales, 0)
        load_halved(nc.sync, out_plane, 0, wb_scales, 1)
        load_halved(nc.sync, out_plane, N, ws_scales, 0)
        load_halved(nc.sync, out_plane, N, ws_scales, 1)
        load_rows(nc.sync, xt_plane, xt_scales, 3)
        lst5 = load_list("lst5", offs5)
        nc.sync.dma_start(wb_w[:].bitcast(I32), words4(wb_words))
        nc.sync.dma_start(ws_w[:].bitcast(I32), words4(ws_words))
        lst3 = load_list("lst3", offs3)
        lst4 = load_list("lst4", offs4)
        lst7 = load_list("lst7", offs7)
        lst6 = load_list("lst6", offs6)
        nc.vector.memset(pages["a", 0][:], 0.0)
        nc.vector.memset(pages["a", 1][:], 0.0)
        nc.vector.memset(pages["b", 0][:], 0.0)
        nc.vector.memset(pages["b", 1][:], 0.0)
        spread(ctx_plane, ctx_stage)
        nc.vector.tensor_copy(wt_g[:], wt_w[:].indirect(lst1[:]))
        for u in range(2):
            nc.vector.tensor_copy(wt_d[u][:], wt_g[:].rearrange("p (c u t) -> p u t c", u=2, t=2)[:, u])
        nc.vector.tensor_copy(wt_gs[:].rearrange("p t c -> p c t"), wt_plane[:].indirect(lst1[:]))
        g0t_ps = ps.tile([P, R], F32, name="g0t_ps", tag="bank_early")
        nc.tensor.matmul_mx(g0t_ps[:], lhsT=xc_w[:].bitcast(E5M2), lhsT_scale=ctx_plane[:, 0, 0:Q],
                            rhs=wg_w[:].bitcast(E4M3), rhs_scale=ctx_plane[:, 0, Q : Q + R], start=True, stop=True)
        nc.scalar.activation(g0t[:], g0t_ps[:].rearrange("q (c t) -> q t c", t=PACK), COPY)
        g0_ps = ps.tile([P, PACK, Q], F32, name="g0_ps")
        for t in range(PACK):
            nc.tensor.transpose(g0_ps[:, t, :], g0t[:, t, :], ident[:])
        nc.scalar.copy(gains[:].rearrange("p (t s) -> p t s", s=2), g0_ps[:, :, 0:Q:64])
        nc.scalar.copy(hid_ctx[:], g0_ps[:].rearrange("p t q -> p q t"))
        lift(out_plane)
        pick_words(x2, lst2[:])
        pick_scales(x2, lst2[:])
        a_ps = []
        for t in range(PACK):
            bank = ps.tile([P, J], F32, name=f"a_ps{t}", tag=f"bank_a{t}")
            nc.tensor.matmul_mx(bank[:], lhsT=wt_d[t // 2][:, t % 2, :].bitcast(E2M1), lhsT_scale=wt_gs[:, t, :],
                                rhs=x2[0][:].bitcast(E5M2), rhs_scale=x2[1][:], start=True, stop=True)
            a_ps.append(bank)
        pick_words(x5, lst5[:])
        pick_scales(x5, lst5[:])
        x5l = (x5[0][:, 0:X], x5[1][:, 0:X])
        x5e = (x5[0][:, X:D], x5[1][:, X:D])
        ctx_q = quantise("ctx", hid_ctx, "wt_d0")
        pe_ps = ps.tile([P, 2, P], F32, name="pe_ps", tag="bank_early")
        for h in range(2):
            short_way(pe_ps[:, h, :], h, x5e)
            output_matrix(pe_ps[:, h, :], h, ctx_q)
        pl_ps = [ps.tile([P, X], F32, name=f"pl_ps{h}") for h in range(2)]
        for h in range(2):
            short_way(pl_ps[h][:], h, x5l)
        a0 = sb.tile([P, J], F32, name="a0", tag="rows0", align_bytes=ALIGN)
        nc.scalar.copy(a0[:], a_ps[0][:])
        a1 = sb.tile([P, J], F32, name="a1", tag="rows1", align_bytes=ALIGN)
        nc.scalar.copy(a1[:], a_ps[1][:])
        a2 = sb.tile([P, J], F32, name="a2", tag="rows2", align_bytes=ALIGN)
        nc.vector.tensor_copy(a2[:], a_ps[2][:])
        a3 = sb.tile([P, J], F32, name="a3", tag="rows3", align_bytes=ALIGN)
        nc.vector.tensor_copy(a3[:], a_ps[3][:])
        for t, a_t in enumerate((a0, a1, a2, a3)):
            nc.scalar.activation(h3[0][:, t, :], a_t[:].indirect(lst3[:]), COPY, scale=gains[:, 2 * t : 2 * t + 1])
        for t, a_t in enumerate((a0, a1, a2, a3)):
            nc.scalar.activation(h3[1][:, t, :], a_t[:].indirect(lst4[:]), COPY, scale=gains[:, 2 * t + 1 : 2 * t + 2])
        p_e = tile("p_e", [P, 2, P], F32)
        nc.vector.tensor_copy(p_e[:], pe_ps[:])
        p_e0 = p_e[:, 0, :]
        p_e1 = p_e[:, 1, :]
        nc.vector.tensor_copy(hid_pl[:, 0:O, :], h3[0][:].rearrange("p t x -> p x t"))
        pl_q = (tile("pl_codes", [P, P], U32), tile("pl_scales", [P, P], U8))
        nc.vector.quantize_mx(pl_q[0][:, 0:O].bitcast(E4M3), pl_q[1][:, 0:O], hid_pl[:, 0:O, :].rearrange("p c t -> p (c t)"))
        nc.vector.tensor_copy(hid_pl[:, O:X, :], h3[1][:].rearrange("p t x -> p x t"))
        nc.vector.quantize_mx(pl_q[0][:, O:X].bitcast(E4M3), pl_q[1][:, O:X], hid_pl[:, O:X, :].rearrange("p c t -> p (c t)"))
        put_v(pages["a", 0], lst6[:, early], p_e0[:])
        put_s(pages["b", 0], lst7[:, early], p_e0[:])
        put_s(pages["b", 1], lst7[:, early], p_e1[:])
        put_s(pages["a", 1], lst6[:, early], p_e1[:])
        for h in range(2):
            output_matrix(pl_ps[h][:], h, pl_q)
        p_l0 = sb.tile([P, P], F32, name="p_l0", tag="p_l0", align_bytes=ALIGN)
        nc.vector.tensor_copy(p_l0[:], pl_ps[0][:])
        p_l1 = sb.tile([P, P], F32, name="p_l1", tag="p_l1", align_bytes=ALIGN)
        nc.vector.tensor_copy(p_l1[:], pl_ps[1][:])
        put_v(pages["a", 0], lst6[:, late], p_l0[:])
        put_s(pages["b", 0], lst7[:, late], p_l0[:])
        put_v(pages["a", 1], lst6[:, late], p_l1[:])
        put_s(pages["b", 1], lst7[:, late], p_l1[:])
        for h in range(2):
            for cols in (slice(0, E // 2), slice(E // 2, E)):
                nc.vector.tensor_tensor(total[h][:, cols], pages["a", h][:, cols], pages["b", h][:, cols], ADD)
                nc.sync.dma_start(out[P * h : P * (h + 1), cols], total[h][:, cols])
